import numpy as np, ml_dtypes
CORES = [24,25,26,27,28,29,30,31]
N = 8
import mx_ref
BF = ml_dtypes.bfloat16
def pick(q, e):
    c = np.concatenate([q[0].reshape(128, -1, 4), np.zeros((128, 1, 4), np.uint8)], axis=1); s = np.concatenate([q[1], np.ones((16, 1), np.uint8)], axis=1)
    return (np.ascontiguousarray(c[:, e].reshape(128, -1)), np.ascontiguousarray(s[:, e]))
def join(*qs):
    return (np.concatenate([q[0] for q in qs], axis=1), np.concatenate([q[1] for q in qs], axis=1))
def put(q, e, v):
    c, s = q[0].reshape(128, -1, 4).copy(), q[1].copy(); c[:, e] = v[0].reshape(128, -1, 4); s[:, e] = v[1]
    return (c.reshape(128, -1), s)
def pk(c, s):
    return (np.ascontiguousarray(c), mx_ref.live(s))
def emit(q):
    return q[0], q[1]
def cols(t, e):
    v = np.concatenate([t.reshape(128, -1, 4), np.zeros((128, 1, 4), BF)], axis=1)
    return np.ascontiguousarray(v[:, e]).reshape(128, -1)
def tile(rs):
    return np.stack(rs, axis=2).reshape(128, -1).astype(BF)
def decode(q):
    o = []
    for b in range(4):
        e = np.zeros((128, 128, 4), np.float32); e[np.arange(128), np.arange(128), b] = 1
        o.append(mx_ref.matmul(mx_ref.quantize(e.reshape(128, 512).astype(BF)), q))
    return np.stack(o, axis=2).reshape(128, -1)
def f(rng, *shape):
    return mx_ref.flush((rng.standard_normal(shape, dtype=np.float32) * np.exp2(rng.integers(-2, 3, shape[:-1] + (1,)))).astype(BF))
def wide(rng, *shape, cols=0):
    v = rng.standard_normal(shape, dtype=np.float32) * np.exp2(rng.integers(-12, 13, shape)).astype(np.float32)
    if cols: v *= np.repeat(np.exp2(rng.integers(-cols, cols + 1, shape[:-2] + (1, shape[-1] // 4))) * (rng.random(shape[:-2] + (1, shape[-1] // 4)) > 0.0625), 4, axis=-1).astype(np.float32)
    return mx_ref.flush(v.astype(BF))
P, K, R = 160, 16, 2
def times(t, v):
    return mx_ref.flush((t.astype(np.float32) * np.asarray(v, np.float32) + np.float32(0)).astype(BF))
def columns(v):
    return mx_ref.flush(np.ascontiguousarray(v.reshape(-1, 128, 4).transpose(1, 0, 2)).reshape(128, -1).astype(np.float32).astype(BF))
def plain(rng):
    return {"x": times(f(rng, N, 128, 4 * P), 64), "u": f(rng, N, 128, 4), "w": f(rng, N, 128, 512)}
def setup_inputs(rng):
    return plain(rng)
def setup_inputs_shadow(rng):
    d, H, xs, us = plain(rng), K // 2, [], []
    for r in range(N):
        way = rng.choice([-1.0, 1.0], 512)
        q = np.where(np.arange(512) < 480, way, 0.0)
        q[480], q[481] = 2.0 ** -14, 2.0 ** -16
        line, at = rng.permutation(480), rng.permutation(P)
        v = rng.standard_normal((P, 512)) * 2.0 ** -4
        v[at[:3 * H + 4 + K]] = 0
        for e, level in ((np.sort(at[:H]), 1.0), (np.sort(at[H:2 * H + 4]), 0.875), (at[2 * H + 4:3 * H + 4], 0.75)):
            for g, j in enumerate(e):
                k = line[16 * (g % H):16 * (g % H) + 16]
                v[j, k] = level * way[k]
                if level > 0.75: v[j, 480], v[j, 481] = 0.25 * (g // 4), 0.25 * (g % 4)
        for j in at[3 * H + 4:3 * H + 4 + K]:
            k = line[16 * H + rng.permutation(480 - 16 * H)[:16]]
            v[j, k] = 0.625 * way[k]
        v = v * rng.choice([-1.0, 1.0], (P, 1))
        xs.append(columns(v * np.exp2(rng.integers(4, 9))))
        us.append(columns(q[None] * np.exp2(rng.integers(-3, 4))))
    return {**d, "x": np.stack(xs), "u": np.stack(us)}
def setup_inputs_ties(rng):
    d = plain(rng)
    d["x"] = np.stack([times(cols(d["x"][r], rng.permutation(np.arange(P) % 6)), np.repeat(rng.choice([-1.0, 1.0], P), 4)) for r in range(N)])
    return d
def setup_inputs_few(rng):
    d = plain(rng)
    n = 8 * rng.integers(K // 8, R * K // 8, N) + rng.integers(4, 8, N)
    p = rng.permutation(N)
    n[p[0]], n[p[1]] = 3, P
    d["x"] = np.stack([times(d["x"][r], 2.0 ** -14 * np.repeat(rng.permutation(P) < n[r], 4)) for r in range(N)])
    return d
def setup_inputs_huge(rng):
    d, xs, us = plain(rng), [], []
    lean = 0.5 + 0.5 * np.sqrt(3.6 / (K - 1))
    for r in range(N):
        way = rng.choice([-1.0, 1.0], 512)
        us.append(columns((way * (1.75 + 0.25 * rng.random(512)) * 2.0 ** 29)[None]))
        v = way * np.where(rng.random((P, 512)) < lean, 1.0, -1.0) * rng.choice([-1.0, 1.0], (P, 1))
        xs.append(columns(v * (1 + rng.random((P, 512))) * 2.0 ** 27))
    return {**d, "x": np.stack(xs), "u": np.stack(us)}
def setup_inputs_spread(rng):
    return {**plain(rng), "x": wide(rng, N, 128, 4 * P, cols=6)}
def check_inputs(d):
    b = []
    for k in ("x", "u", "w"):
        v = np.abs(d[k].astype(np.float32))
        if not (np.isfinite(v).all() and ((v == 0) | (v >= 2.0 ** -30) & (v <= 2.0 ** 30)).all()): b.append("a value of " + k)
    return b
UP = 2.0 ** np.arange(-64, 74)
DOWN = 2.0 ** -np.arange(-64.0, 74)
def play(x, u):
    ask = [mx_ref.quantize(np.concatenate([u[r], np.zeros((128, 508), BF)], axis=1)) for r in range(N)]
    X = mx_ref.quantize(np.concatenate([x[r] for r in range(N)], axis=1))
    free, rounds = np.ones((N, P), bool), []
    for t in range(R):
        at, took = np.full(128, -1), np.zeros((N, K), int)
        for r in range(N):
            s = np.abs(mx_ref.matmul(ask[r], pick(X, P * r + np.arange(P)))[0])
            o = np.argsort(np.where(free[r], 0.0 - s, np.inf), kind="stable")[:K]
            free[r, o] = False
            at[r * K:r * K + K] = P * r + o
            took[r] = o
        m = pick(X, at)
        rounds.append((took, m))
        d = np.diagonal(mx_ref.matmul(m, m))
        h = np.where(d > 0, DOWN[np.maximum(np.searchsorted(UP, d, side="right") - 1, 0)], 0.0).astype(np.float32)
        c = np.zeros((128, N * P, 4), np.float32)
        c[:, :, 0] = mx_ref.matmul(m, X) * h[:, None]
        c = mx_ref.quantize(c.reshape(128, -1).astype(BF))
        dx, parts = decode(X).reshape(128, N * P, 4), []
        dm = np.concatenate([dx, np.zeros((128, 1, 4), np.float32)], axis=1)[:, at]
        for b in range(4):
            mt = np.zeros((128, 128, 4), np.float32)
            mt[:, :, 0] = dm[:, :, b].T
            z = mx_ref.matmul(mx_ref.quantize(mt.reshape(128, 512).astype(BF)), c)
            parts.append(dx[:, :, b] - np.float32(0.25) * z)
        X = mx_ref.quantize(tile(parts))
    return X, rounds
def reference(x, u, w):
    y, pl = np.zeros((N, 128, R * N * K), np.float32), np.zeros((N, 1, R * K), np.float32)
    oc, osc = np.zeros((N, 128, 4 * P), np.uint8), np.zeros((N, 16, P), np.uint8)
    own = [mx_ref.quantize(np.ascontiguousarray(w[r])) for r in range(N)]
    X, rounds = play(x, u)
    for t in range(R):
        took, m = rounds[t]
        for r in range(N):
            pl[r, 0, t * K:t * K + K] = took[r]
            y[r, :, t * N * K:(t + 1) * N * K] = mx_ref.matmul(own[r], m)[:, :N * K]
    for r in range(N):
        oc[r], osc[r] = emit(pick(X, P * r + np.arange(P)))
    return {"y": y, "pl": pl, "oc": oc, "osc": osc}

@@ -1,0 +1,331 @@
+from concourse.bass import DstId, RemoteDMATransfer
+from concourse.mybir import dt, AluOpType, AxisListType, ActivationFunctionType
+
+P, K, R, N = 160, 16, 2, 8
+STEP = 512
+OUT = STEP * K
+LO, HI = -64, 72
+NT = HI - LO
+GRID = False
+
+BF, F32, Q4, U8 = "bfloat16", "float32", "float8_e4m3fn_x4", "uint8"
+SCRATCH = {
+    "xt": ("sbuf", [128, 4 * P], BF), "ub": ("sbuf", [128, 8], BF), "wt": ("sbuf", [128, 512], BF),
+    "zb": ("sbuf", [128, 528], BF), "jp": ("sbuf", [128, 128], BF), "ut": ("sbuf", [128, 512], BF),
+    "cmp": ("sbuf", [128, 4 * P], BF), "wr": ("sbuf", [128, 512], BF), "em": ("sbuf", [128, 528], BF),
+    "th0": ("sbuf", [128, P], BF), "th1": ("sbuf", [128, P], BF),
+    "nf0": ("sbuf", [128, 4], F32), "nf1": ("sbuf", [128, 4], F32),
+    "ar": ("sbuf", [128, P], F32), "ac": ("sbuf", [128, 4], F32), "sg": ("sbuf", [128, P], BF),
+    "pc0": ("sbuf", [128, 4], F32), "pc1": ("sbuf", [128, 4], F32),
+    "off0": ("sbuf", [128, 8], "uint16"), "off1": ("sbuf", [128, 8], "uint16"),
+    "eye": ("sbuf", [128, 128], BF), "two": ("sbuf", [128, NT], BF), "up": ("sbuf", [128, NT], BF),
+    "dg": ("sbuf", [128, 128], F32), "dd": ("sbuf", [128, 4], F32), "hm": ("sbuf", [128, NT], BF),
+    "hh": ("sbuf", [128, NT], F32),
+    "mt": ("sbuf", [128, 1024], BF), "ct": ("sbuf", [128, 4 * P], BF), "rt": ("sbuf", [128, 4 * P], BF),
+    "ys0": ("sbuf", [128, 128], F32), "ys1": ("sbuf", [128, 128], F32),
+    "pu0": ("psum", [128, 512], F32), "pu1": ("psum", [128, 512], F32), "pu2": ("psum", [128, 512], F32),
+    "pr0": ("psum", [128, 512], F32), "pr1": ("psum", [128, 512], F32), "pm": ("psum", [128, 512], F32),
+    "pg": ("psum", [128, 512], F32), "pt": ("psum", [128, 512], F32),
+}
+for _n, _w in (("x0", P), ("x1", P), ("x2", P), ("m0", 128), ("m1", 128), ("uu", 128), ("ww", 128), ("wk", 128),
+               ("kk", P), ("ee", 512), ("tt", 512), ("cc", P)):
+    SCRATCH[_n + "q"] = ("sbuf", [128, _w], Q4)
+    SCRATCH[_n + "s"] = ("sbuf", [128, _w], U8)
+
+SEMAPHORES = ["arr0", "arr1", "far0", "far1", "sent"] + ["s%d" % i for i in range(140)]
+
+
+def mask_of(engines):
+    m = 0
+    for e in engines:
+        m |= 1 << e
+    return m
+
+
+def rank_program(g, core, T, topo):
+    rank = T.rank_of(core)
+    if rank is None:
+        return
+    A, F = AluOpType, ActivationFunctionType
+    V, S, PE, Y = g.vector, g.scalar, g.tensor, g.sync
+    used = [0]
+    open_marks = {}
+
+    def mark(ins, n=1, into=None):
+        if into is None:
+            into = ["s%d" % used[0], 0]
+            used[0] += 1
+        ins.then_inc(T.sem[into[0]], n)
+        into[1] += n
+        open_marks[into[0]] = into
+        return into
+
+    def wait(q, *marks):
+        for m in marks:
+            if m is not None:
+                q.wait_ge(T.sem[m[0]], m[1])
+                open_marks.pop(m[0], None)
+
+    def pair(name, a=None, b=None):
+        return T[name + "q"][:, a:b], T[name + "s"][:, a:b]
+
+    def quant(name, a, b, src):
+        q, s = pair(name, a, b)
+        return V.quantize_mx(q, s, src)
+
+    def mm(out, w, x, start=True, stop=True):
+        return PE.matmul_mx(out, w[0], w[1], x[0], x[1], start, stop)
+
+    def count(out, pattern, base, step):
+        m = mark(g.iota(out, pattern, base, step, allow_small_or_imprecise_dtypes=True))
+        wait(g, m)
+        return m
+
+    def put(dsts, src, engines, sem):
+        ids = []
+        for c in dsts:
+            rid, pid, _ = topo.addr(c)
+            ids.append(DstId(rid=rid, pnc=pid))
+        tr = RemoteDMATransfer(dst_ids=ids, dma_engine_mask=mask_of(engines), remote_sem=sem, src=src,
+                               dsts=[src for _ in dsts])
+        g.remote_dma_fused([tr], local_sem=T.sem.sent)
+        return len(engines)
+
+    cores = list(T.cores)
+    others = [cores[(rank + i) % N] for i in range(1, N)]
+    engines = [e for e in topo.engines(core, others[0]) if all(e in topo.engines(core, c) for c in others)]
+    half = len(engines) // 2
+    near = [c for c in others if topo.die(c) == topo.die(core)]
+    block = sorted(T.rank_of(c) for c in near + [core])
+    sent = [0]
+
+    u_in = mark(S.dma_start(T.ub[:, 0:4], T.u[:]), 16)
+    x_in = mark(Y.dma_start(T.xt[:], T.x[:]), 16)
+    wait(Y, x_in)
+    w_in = mark(Y.dma_start(T.wt[:], T.w[:]), 16)
+
+    zb = mark(V.memset(T.zb[:], 0.0))
+    jp = count(T.jp[:], [[1, 128]], 0, -1)
+    wz = mark(V.memset(T.wr[:, 2:512:4], 0.0))
+    mark(V.memset(T.wr[:, 3:512:4], 0.0), into=wz)
+    wr = mark(V.memset(T.wr[:, 0:512:4], float(STEP)))
+    mark(V.memset(T.wr[:, 1:512:4], float(STEP)), into=wr)
+    rows = mark(V.memset(T.cmp[0:64, 2:4 * P:4], 1.0))
+    mark(V.memset(T.cmp[0:64, 3:4 * P:4], 1.0), into=rows)
+    wait(g, wz)
+    krow = count(T.wr[0:1, 2:512:4], [[0, 128 // K], [-STEP, K]], OUT, 0)
+    high = count(T.cmp[64:128, 2:4 * P:4], [[1, P // 16], [0, 16]], 0, 0)
+    low = count(T.cmp[64:128, 3:4 * P:4], [[0, P // 16], [1, 16]], 0, 0)
+    wait(g, zb)
+    em = mark(g.affine_select(T.em[:, 0:516], T.zb[:, 0:516], [[1, 516]], A.not_equal, -4.0, -3, -4))
+    wait(V, jp)
+    le = mark(V.tensor_scalar(T.th0[:, 0:128], T.jp[:], 0.0, None, A.is_le))
+    nf = mark(V.tensor_scalar(T.nf0[:, 0:2], T.jp[:, 0:97:96], 0.0, None, A.is_gt))
+    wait(V, wz)
+    mark(V.memset(T.wr[0:1, 3:512:4], float(-OUT)), into=wr)
+    mark(V.memset(T.wr[64:65, 2:512:4], 16.0), into=wr)
+    mark(V.memset(T.wr[64:65, 3:512:4], 1.0), into=wr)
+    wait(V, le, nf)
+    th = mark(V.tensor_scalar(T.th0[:, 128:P], T.th0[:, 96:128], T.nf0[:, 1:2], T.nf0[:, 1:2], A.add, A.add))
+    wait(V, wr, krow)
+    wk = mark(quant("wk", 0, 128, T.wr[:]))
+
+    wait(S, zb)
+    mz = mark(S.activation(T.mt[:, 0:512], T.zb[:, 0:512], F.Copy))
+    mark(S.activation(T.mt[:, 512:1024], T.zb[:, 0:512], F.Copy), into=mz)
+
+    wait(S, u_in)
+    ut = mark(S.activation(T.ut[:, 0:512:4], T.zb[:, 0:128], F.Identity, bias=T.ub[:, 0:1]))
+    mark(S.activation(T.ut[:, 1:512:4], T.zb[:, 0:128], F.Identity, bias=T.ub[:, 1:2]), into=ut)
+    wait(V, zb, u_in)
+    mark(V.tensor_scalar(T.ut[:, 2:512:4], T.zb[:, 0:128], T.ub[:, 2:3], None, A.add), into=ut)
+    mark(V.tensor_scalar(T.ut[:, 3:512:4], T.zb[:, 0:128], T.ub[:, 3:4], None, A.add), into=ut)
+    wait(V, ut)
+    uq = mark(quant("uu", 0, 128, T.ut[:]))
+    wait(V, rows, high, low)
+    wait(V, x_in)
+    xq = mark(quant("x0", 0, P, T.xt[:]))
+    wait(PE, uq, wk)
+
+    stores = []
+    u_free = []
+    for t in range(R):
+        xn, mn = "x%d" % t, "m%d" % t
+        thr, nfb, pc, off = T["th%d" % t], T["nf%d" % t], T["pc%d" % t], T["off%d" % t]
+        first = t == 0
+
+        wait(PE, *u_free)
+        wait(PE, xq)
+        row = mark(mm(T.pu0[:, 0:P], pair("uu"), pair(xn)))
+        ca = mark(mm(T.pu1[:, 0:128], pair(xn, 0, 128), pair("uu")))
+        cb = mark(mm(T.pu2[:, 0:128], pair(xn, 32, P), pair("uu")))
+        wait(S, row)
+        ar = mark(S.activation(T.ar[:], T.pu0[:, 0:P], F.Abs))
+        if first:
+            wait(V, th)
+        wait(V, ca)
+        aa = mark(V.tensor_scalar(T.ac[:, 0:1], T.pu1[:, 0:1], -1.0, T.pu1[:, 0:1], A.mult, A.max))
+        wait(V, cb)
+        ab = mark(V.tensor_scalar(T.ac[:, 1:2], T.pu2[:, 0:1], -1.0, T.pu2[:, 0:1], A.mult, A.max))
+
+        wait(S, aa, ar)
+        sg = mark(S.activation(T.sg[:, 0:128], T.ar[:, 0:128], F.Sign, bias=T.ac[:, 0:1], scale=-1.0))
+        wait(S, ab)
+        mark(S.activation(T.sg[:, 128:P], T.ar[:, 128:P], F.Sign, bias=T.ac[:, 1:2], scale=-1.0), into=sg)
+        wait(V, aa, ar, ab)
+        cm = mark(V.tensor_scalar(T.cmp[:, 1:512:4], T.ar[:, 0:128], T.ac[:, 1:2], nfb[:, 1:2], A.is_lt, A.is_gt))
+        mark(V.tensor_scalar(T.cmp[:, 513:4 * P:4], T.ar[:, 128:P], T.ac[:, 0:1], nfb[:, 0:1], A.is_le, A.is_gt), into=cm)
+        wait(V, sg)
+        mark(V.tensor_tensor(T.cmp[:, 0:4 * P:4], T.sg[:], thr[:], A.is_ge), into=cm)
+        wait(V, cm)
+        kq = mark(quant("kk", 0, P, T.cmp[:]))
+        wait(PE, kq)
+        z = mark(mm(T.pu0[:, 0:P], pair("wk"), pair("kk")))
+        if first:
+            za = mark(mm(T.pu1[:, 0:128], pair("kk", 0, 128), pair("wk")))
+            zc = mark(mm(T.pu2[:, 0:128], pair("kk", 32, P), pair("wk")))
+        wait(V, z)
+        pl = mark(V.tensor_reduce(pc[:, 0:1], T.pu0[:, 0:P], AxisListType.X, A.min, apply_absolute_value=True))
+        wait(V, pl)
+        of = mark(V.tensor_copy(off[:, 0:1], pc[:, 0:1]))
+
+        a, b = K * rank, K * rank + K
+        mq, ms = pair(mn, a, b)
+        wait(S, of)
+        gs = mark(S.activation(ms, T[xn + "s"][:, 0:P].indirect(off[:, 0:1]), F.Copy))
+        wait(V, of)
+        gq = mark(V.tensor_copy(mq.bitcast(dt.uint32), T[xn + "q"][:, 0:P].bitcast(dt.uint32).indirect(off[:, 0:1])))
+        e_s, e_q = (engines[:half], engines[half:]) if first else (engines, engines)
+        to = near if GRID else others
+        arr = T.sem["arr%d" % t]
+        if first:
+            wait(g, em)
+        wait(g, gq)
+        sent[0] += put(to, mq.bitcast(dt.uint8), e_q, arr)
+        wait(g, gs)
+        sent[0] += put(to, ms, e_s, arr)
+        landed = ["arr%d" % t, len(to) * (len(e_s) + len(e_q))]
+        if GRID:
+            wait(g, landed)
+            mate = [cores[(rank + len(block)) % N]]
+            bq, bs = pair(mn, K * block[0], K * (block[-1] + 1))
+            far = T.sem["far%d" % t]
+            n = put(mate, bq.bitcast(dt.uint8), engines[half:], far) + put(mate, bs, engines[:half], far)
+            sent[0] += n
+            beyond = ["far%d" % t, n]
+        else:
+            beyond = None
+
+        if first:
+            wait(V, em)
+            eq = mark(quant("ee", 0, 128, T.em[:, 3:515]))
+            for j in range(1, 4):
+                mark(quant("ee", 128 * j, 128 * j + 128, T.em[:, 3 - j:515 - j]), into=eq)
+            two = mark(V.memset(T.two[:], 2.0))
+            tab = mark(V.tensor_scalar(T.eye[:], T.jp[:], 0.0, None, A.is_equal))
+            wait(V, two)
+            mark(V.tensor_tensor_scan(T.up[:], T.two[:], T.zb[:, 0:NT], 2.0 ** LO, A.mult, A.add), into=tab)
+            wait(V, w_in)
+            wq = mark(quant("ww", 0, 128, T.wt[:]))
+            cz = mark(S.activation(T.ct[:, 0:512], T.zb[:, 0:512], F.Copy))
+            mark(S.activation(T.ct[:, 512:4 * P], T.zb[:, 0:4 * P - 512], F.Copy), into=cz)
+            rows = mark(V.tensor_scalar(T.cmp[0:1, 3:4 * P:4], T.pu0[0:1, 0:P], float(OUT), None, A.is_ge))
+            wait(V, za)
+            nf = mark(V.tensor_scalar(T.nf1[:, 0:1], T.pu1[:, 0:1], float(OUT), None, A.is_lt))
+            wait(V, zc)
+            mark(V.tensor_scalar(T.nf1[:, 1:2], T.pu2[:, 0:1], float(OUT), T.nf0[:, 1:2], A.is_lt, A.max), into=nf)
+            wait(V, nf)
+            th = mark(V.tensor_scalar(T.th1[:, 0:128], T.th0[:, 0:128], T.nf1[:, 0:1], T.nf1[:, 0:1], A.add, A.add))
+            mark(V.tensor_scalar(T.th1[:, 128:P], T.th0[:, 96:128], T.nf1[:, 1:2], T.nf1[:, 1:2], A.add, A.add), into=th)
+            wait(V, tab, rows, th)
+            wait(PE, eq)
+            wait(S, mz, cz)
+        banks = [T.pr0, T.pr1, T.pm, T.pg]
+
+        def decode(j):
+            mm(banks[j][:, 0:P], pair("ee", 128 * j, 128 * j + 128), pair(xn), True, False)
+
+        decode(0)
+        decode(1)
+        if first:
+            wait(PE, wq, nf)
+
+        wait(PE, gq, gs, landed, beyond)
+        mmx = mark(mm(T.pm[:, 0:128], pair(mn), pair(mn)))
+        mtp = mark(mm(T.pt[:, 0:512], pair(mn), pair("ee")))
+        gp = mark(mm(T.pg[:, 0:P], pair(mn), pair(xn)))
+        yp = mark(mm(T.pu1[:, 0:128], pair("ww"), pair(mn)))
+
+        wait(V, mmx)
+        dg = mark(V.tensor_tensor(T.dg[:], T.pm[:, 0:128], T.eye[:], A.mult))
+        wait(V, dg)
+        dd = mark(V.tensor_reduce(T.dd[:, 0:1], T.dg[:], AxisListType.X, A.add))
+        wait(V, dd)
+        hm = mark(V.tensor_scalar(T.hm[:], T.up[:], T.dd[:, 0:1], 0.5, A.is_gt, A.max))
+        wait(V, hm)
+        hh = mark(V.tensor_tensor_scan(T.hh[:], T.hm[:], T.zb[:, 0:NT], 2.0 ** -LO, A.mult, A.add))
+        wait(PE, dg)
+        decode(2)
+
+        def turn(j):
+            o = 512 * (j % 2)
+            return mark(S.activation(T.mt[:, o:o + 512:4], T.pt[:, 128 * j:128 * j + 128], F.Copy, scale=-0.25))
+
+        def pack(j, made):
+            o = 512 * (j % 2)
+            wait(V, made)
+            return mark(quant("tt", 128 * j, 128 * j + 128, T.mt[:, o:o + 512]))
+
+        wait(S, mtp)
+        m0 = turn(0)
+        m1 = turn(1)
+        wait(S, gp, hh)
+        ct = mark(S.activation(T.ct[:, 0:4 * P:4], T.pg[:, 0:P], F.Copy, scale=T.hh[:, NT - 1:NT]))
+        wait(PE, ct)
+        decode(3)
+        q0 = pack(0, m0)
+        q1 = pack(1, m1)
+        wait(V, ct)
+        cq = mark(quant("cc", 0, P, T.ct[:]))
+        wait(S, q0)
+        m2 = turn(2)
+        wait(S, q1)
+        m3 = turn(3)
+        q2 = pack(2, m2)
+        q3 = pack(3, m3)
+        ys = T["ys%d" % t]
+        wait(S, yp)
+        yc = mark(S.activation(ys[:], T.pu1[:, 0:128], F.Copy))
+        wait(Y, pl, landed, beyond)
+        stores.append((Y, mark(Y.dma_start(T.pl[0:1, K * t:K * t + K], pc[0:K, 0:1]), 16)))
+        wait(Y, yc)
+        stores.append((Y, mark(Y.dma_start(T.y[:, 128 * t:128 * t + 128], ys[:]), 16)))
+
+        wait(PE, q0, q1, cq)
+        made = None
+        for j, qj in enumerate((None, None, q2, q3)):
+            wait(PE, qj)
+            zj = mark(mm(banks[j][:, 0:P], pair("tt", 128 * j, 128 * j + 128), pair("cc"), False, True))
+            out = T.rt[:, j:4 * P:4]
+            if j % 2 == 0:
+                wait(S, zj)
+                made = mark(S.activation(out, banks[j][:, 0:P], F.Copy, scale=-0.25), into=made)
+            else:
+                wait(V, zj)
+                made = mark(V.tensor_scalar(out, banks[j][:, 0:P], -0.25, None, A.mult), into=made)
+        wait(V, made)
+        xq = mark(quant("x%d" % (t + 1), 0, P, T.rt[:]))
+        u_free = [rows, yc, m3] if first else []
+
+    wait(Y, xq)
+    wait(S, xq)
+    last_q, last_s = T["x%dq" % R], T["x%ds" % R]
+    stores.append((Y, mark(Y.dma_start(T.oc[:], last_q[:].bitcast(dt.uint8)), 16)))
+    for k in range(4):
+        q = S if k < 3 else Y
+        stores.append((q, mark(q.dma_start(T.osc[4 * k:4 * k + 4, :], last_s[32 * k:32 * k + 4, :]), 16)))
+    g.wait_ge(T.sem.sent, sent[0])
+    for q, m in stores:
+        wait(q, m)
+    for m in list(open_marks.values()):
+        wait(g, m)

@@ -6,33 +6,34 @@ STEP = 512
 OUT = STEP * K
 LO, HI = -64, 72
 NT = HI - LO
-GRID = False
+DIRECT = True
+SPLIT = False
 
 BF, F32, Q4, U8 = "bfloat16", "float32", "float8_e4m3fn_x4", "uint8"
 SCRATCH = {
     "xt": ("sbuf", [128, 4 * P], BF), "ub": ("sbuf", [128, 8], BF), "wt": ("sbuf", [128, 512], BF),
     "zb": ("sbuf", [128, 528], BF), "jp": ("sbuf", [128, 128], BF), "ut": ("sbuf", [128, 512], BF),
     "cmp": ("sbuf", [128, 4 * P], BF), "wr": ("sbuf", [128, 512], BF), "em": ("sbuf", [128, 528], BF),
-    "th0": ("sbuf", [128, P], BF), "th1": ("sbuf", [128, P], BF),
+    "cl": ("sbuf", [128, 2 * P], BF), "ch": ("sbuf", [128, 2 * P], BF),
     "nf0": ("sbuf", [128, 4], F32), "nf1": ("sbuf", [128, 4], F32),
-    "ar": ("sbuf", [128, P], F32), "ac": ("sbuf", [128, 4], F32), "sg": ("sbuf", [128, P], BF),
+    "ar": ("sbuf", [128, P], F32), "ac": ("sbuf", [128, 4], F32),
     "pc0": ("sbuf", [128, 4], F32), "pc1": ("sbuf", [128, 4], F32),
     "off0": ("sbuf", [128, 8], "uint16"), "off1": ("sbuf", [128, 8], "uint16"),
     "eye": ("sbuf", [128, 128], BF), "two": ("sbuf", [128, NT], BF), "up": ("sbuf", [128, NT], BF),
-    "dg": ("sbuf", [128, 128], F32), "dd": ("sbuf", [128, 4], F32), "hm": ("sbuf", [128, NT], BF),
-    "hh": ("sbuf", [128, NT], F32),
-    "mt": ("sbuf", [128, 1024], BF), "ct": ("sbuf", [128, 4 * P], BF), "rt": ("sbuf", [128, 4 * P], BF),
+    "dg": ("sbuf", [128, 64], F32), "dd": ("sbuf", [128, 4], F32), "hm": ("sbuf", [128, NT], BF),
+    "hh": ("sbuf", [128, NT // 2], F32),
+    "mt": ("sbuf", [128, 2048], BF), "ct": ("sbuf", [128, 4 * P], BF), "rt": ("sbuf", [128, 4 * P], BF),
     "ys0": ("sbuf", [128, 128], F32), "ys1": ("sbuf", [128, 128], F32),
-    "pu0": ("psum", [128, 512], F32), "pu1": ("psum", [128, 512], F32), "pu2": ("psum", [128, 512], F32),
-    "pr0": ("psum", [128, 512], F32), "pr1": ("psum", [128, 512], F32), "pm": ("psum", [128, 512], F32),
-    "pg": ("psum", [128, 512], F32), "pt": ("psum", [128, 512], F32),
+    "pa": ("psum", [128, 512], F32), "pb": ("psum", [128, 512], F32), "pc": ("psum", [128, 512], F32),
+    "pd": ("psum", [128, 512], F32), "pr0": ("psum", [128, 512], F32), "pr1": ("psum", [128, 512], F32),
+    "pr2": ("psum", [128, 512], F32), "pr3": ("psum", [128, 512], F32),
 }
 for _n, _w in (("x0", P), ("x1", P), ("x2", P), ("m0", 128), ("m1", 128), ("uu", 128), ("ww", 128), ("wk", 128),
                ("kk", P), ("ee", 512), ("tt", 512), ("cc", P)):
     SCRATCH[_n + "q"] = ("sbuf", [128, _w], Q4)
     SCRATCH[_n + "s"] = ("sbuf", [128, _w], U8)
 
-SEMAPHORES = ["arr0", "arr1", "far0", "far1", "sent"] + ["s%d" % i for i in range(140)]
+SEMAPHORES = ["arr0", "arr1", "sent"] + ["s%d" % i for i in range(140)]
 
 
 def mask_of(engines):
@@ -81,227 +82,214 @@ def rank_program(g, core, T, topo):
         wait(g, m)
         return m
 
-    def put(dsts, src, engines, sem):
-        ids = []
-        for c in dsts:
-            rid, pid, _ = topo.addr(c)
-            ids.append(DstId(rid=rid, pnc=pid))
-        tr = RemoteDMATransfer(dst_ids=ids, dma_engine_mask=mask_of(engines), remote_sem=sem, src=src,
-                               dsts=[src for _ in dsts])
-        g.remote_dma_fused([tr], local_sem=T.sem.sent)
-        return len(engines)
-
     cores = list(T.cores)
     others = [cores[(rank + i) % N] for i in range(1, N)]
     engines = [e for e in topo.engines(core, others[0]) if all(e in topo.engines(core, c) for c in others)]
     half = len(engines) // 2
-    near = [c for c in others if topo.die(c) == topo.die(core)]
-    block = sorted(T.rank_of(c) for c in near + [core])
     sent = [0]
+
+    def put(dsts, src, sem, use):
+        ids = []
+        for c in dsts:
+            rid, pid, _ = topo.addr(c)
+            ids.append(DstId(rid=rid, pnc=pid))
+        tr = RemoteDMATransfer(dst_ids=ids, dma_engine_mask=mask_of(use), remote_sem=T.sem[sem], src=src,
+                               dsts=[src for _ in dsts])
+        g.remote_dma_fused([tr], local_sem=T.sem.sent)
+        sent[0] += len(use)
+        return len(dsts) * len(use)
 
     u_in = mark(S.dma_start(T.ub[:, 0:4], T.u[:]), 16)
     x_in = mark(Y.dma_start(T.xt[:], T.x[:]), 16)
     wait(Y, x_in)
     w_in = mark(Y.dma_start(T.wt[:], T.w[:]), 16)
 
+    wz = mark(V.memset(T.wr[:, 3:512:4], 0.0))
     zb = mark(V.memset(T.zb[:], 0.0))
     jp = count(T.jp[:], [[1, 128]], 0, -1)
-    wz = mark(V.memset(T.wr[:, 2:512:4], 0.0))
-    mark(V.memset(T.wr[:, 3:512:4], 0.0), into=wz)
-    wr = mark(V.memset(T.wr[:, 0:512:4], float(STEP)))
+    wr = mark(V.memset(T.wr[:, 0:512:4], 0.0))
     mark(V.memset(T.wr[:, 1:512:4], float(STEP)), into=wr)
-    rows = mark(V.memset(T.cmp[0:64, 2:4 * P:4], 1.0))
-    mark(V.memset(T.cmp[0:64, 3:4 * P:4], 1.0), into=rows)
-    wait(g, wz)
-    krow = count(T.wr[0:1, 2:512:4], [[0, 128 // K], [-STEP, K]], OUT, 0)
-    high = count(T.cmp[64:128, 2:4 * P:4], [[1, P // 16], [0, 16]], 0, 0)
-    low = count(T.cmp[64:128, 3:4 * P:4], [[0, P // 16], [1, 16]], 0, 0)
-    wait(g, zb)
-    em = mark(g.affine_select(T.em[:, 0:516], T.zb[:, 0:516], [[1, 516]], A.not_equal, -4.0, -3, -4))
-    wait(V, jp)
-    le = mark(V.tensor_scalar(T.th0[:, 0:128], T.jp[:], 0.0, None, A.is_le))
-    nf = mark(V.tensor_scalar(T.nf0[:, 0:2], T.jp[:, 0:97:96], 0.0, None, A.is_gt))
+    mark(V.memset(T.wr[:, 2:512:4], float(STEP)), into=wr)
     wait(V, wz)
+    w2 = mark(V.memset(T.wr[64:66, 3:512:4], 16.0 * STEP))
+    mark(V.memset(T.wr[96:98, 3:512:4], float(STEP)), into=w2)
     mark(V.memset(T.wr[0:1, 3:512:4], float(-OUT)), into=wr)
-    mark(V.memset(T.wr[64:65, 2:512:4], 16.0), into=wr)
-    mark(V.memset(T.wr[64:65, 3:512:4], 1.0), into=wr)
-    wait(V, le, nf)
-    th = mark(V.tensor_scalar(T.th0[:, 128:P], T.th0[:, 96:128], T.nf0[:, 1:2], T.nf0[:, 1:2], A.add, A.add))
-    wait(V, wr, krow)
-    wk = mark(quant("wk", 0, 128, T.wr[:]))
+    rows = mark(V.memset(T.cmp[0:64, 3:4 * P:4], 1.0))
+    wait(g, wz)
+    krow = count(T.wr[32:33, 3:512:4], [[0, 128 // K], [-STEP, K]], OUT, 0)
+    high = count(T.cmp[64:96, 3:4 * P:4], [[1, P // 16], [0, 16]], 0, 0)
+    low = count(T.cmp[96:128, 3:4 * P:4], [[0, P // 16], [1, 16]], 0, 0)
+    lo = mark(V.memset(T.cl[:, 0:2 * P:2], 2.0))
+    mark(V.memset(T.cl[0:64, 257:2 * P:2], -1.5), into=lo)
+    wait(V, jp)
+    mark(V.tensor_scalar(T.cl[:, 1:256:2], T.jp[:], 0.0, -1.0, A.is_gt, A.mult), into=lo)
+    mark(V.tensor_scalar(T.cl[64:128, 257:2 * P:2], T.jp[64:128, 96:128], 0.0, -1.0, A.is_gt, A.mult), into=lo)
+    mark(V.tensor_scalar(T.nf0[:, 0:2], T.jp[:, 0:97:96], 0.0, None, A.is_gt), into=lo)
+
+    def upper(nfb):
+        m = mark(V.tensor_scalar(T.ch[:, 1:256:2], T.cl[:, 1:256:2], nfb[:, 0:1], 1.0, A.subtract, A.add))
+        return mark(V.tensor_scalar(T.ch[:, 257:2 * P:2], T.cl[:, 257:2 * P:2], nfb[:, 1:2], 1.0, A.subtract, A.add), into=m)
 
     wait(S, zb)
-    mz = mark(S.activation(T.mt[:, 0:512], T.zb[:, 0:512], F.Copy))
-    mark(S.activation(T.mt[:, 512:1024], T.zb[:, 0:512], F.Copy), into=mz)
+    ez = mark(S.activation(T.em[:, 0:516], T.zb[:, 0:516], F.Copy))
 
     wait(S, u_in)
     ut = mark(S.activation(T.ut[:, 0:512:4], T.zb[:, 0:128], F.Identity, bias=T.ub[:, 0:1]))
-    mark(S.activation(T.ut[:, 1:512:4], T.zb[:, 0:128], F.Identity, bias=T.ub[:, 1:2]), into=ut)
     wait(V, zb, u_in)
-    mark(V.tensor_scalar(T.ut[:, 2:512:4], T.zb[:, 0:128], T.ub[:, 2:3], None, A.add), into=ut)
-    mark(V.tensor_scalar(T.ut[:, 3:512:4], T.zb[:, 0:128], T.ub[:, 3:4], None, A.add), into=ut)
+    for j in range(1, 4):
+        mark(V.tensor_scalar(T.ut[:, j:512:4], T.zb[:, 0:128], T.ub[:, j:j + 1], None, A.add), into=ut)
+    wait(V, w2)
+    mark(V.memset(T.wr[64:65, 3:512:4], 16.0), into=wr)
+    mark(V.memset(T.wr[96:97, 3:512:4], 1.0), into=wr)
     wait(V, ut)
     uq = mark(quant("uu", 0, 128, T.ut[:]))
-    wait(V, rows, high, low)
     wait(V, x_in)
     xq = mark(quant("x0", 0, P, T.xt[:]))
-    wait(PE, uq, wk)
+    wait(PE, uq)
+    wait(V, lo)
+    hi = upper(T.nf0)
+    wait(V, wr, krow)
+    wk = mark(quant("wk", 0, 128, T.wr[:]))
 
     stores = []
-    u_free = []
+    banks = [T.pr0, T.pr1, T.pr2, T.pr3]
+    yc = None
     for t in range(R):
         xn, mn = "x%d" % t, "m%d" % t
-        thr, nfb, pc, off = T["th%d" % t], T["nf%d" % t], T["pc%d" % t], T["off%d" % t]
+        nfb, pc, off = T["nf%d" % t], T["pc%d" % t], T["off%d" % t]
         first = t == 0
 
-        wait(PE, *u_free)
         wait(PE, xq)
-        row = mark(mm(T.pu0[:, 0:P], pair("uu"), pair(xn)))
-        ca = mark(mm(T.pu1[:, 0:128], pair(xn, 0, 128), pair("uu")))
-        cb = mark(mm(T.pu2[:, 0:128], pair(xn, 32, P), pair("uu")))
+        row = mark(mm(T.pb[:, 0:P], pair("uu"), pair(xn)))
+        ca = mark(mm(T.pc[:, 0:128], pair(xn, 0, 128), pair("uu")))
+        cb = mark(mm(T.pd[:, 0:128], pair(xn, 32, P), pair("uu")))
         wait(S, row)
-        ar = mark(S.activation(T.ar[:], T.pu0[:, 0:P], F.Abs))
-        if first:
-            wait(V, th)
+        ar = mark(S.activation(T.ar[:], T.pb[:, 0:P], F.Abs))
         wait(V, ca)
-        aa = mark(V.tensor_scalar(T.ac[:, 0:1], T.pu1[:, 0:1], -1.0, T.pu1[:, 0:1], A.mult, A.max))
+        aa = mark(V.tensor_scalar(T.ac[:, 0:1], T.pc[:, 0:1], -1.0, T.pc[:, 0:1], A.mult, A.max))
         wait(V, cb)
-        ab = mark(V.tensor_scalar(T.ac[:, 1:2], T.pu2[:, 0:1], -1.0, T.pu2[:, 0:1], A.mult, A.max))
+        ab = mark(V.tensor_scalar(T.ac[:, 1:2], T.pd[:, 0:1], -1.0, T.pd[:, 0:1], A.mult, A.max))
 
         wait(S, aa, ar)
-        sg = mark(S.activation(T.sg[:, 0:128], T.ar[:, 0:128], F.Sign, bias=T.ac[:, 0:1], scale=-1.0))
+        sg = mark(S.activation(T.ch[:, 0:256:2], T.ar[:, 0:128], F.Sign, bias=T.ac[:, 0:1], scale=-1.0))
         wait(S, ab)
-        mark(S.activation(T.sg[:, 128:P], T.ar[:, 128:P], F.Sign, bias=T.ac[:, 1:2], scale=-1.0), into=sg)
-        wait(V, aa, ar, ab)
-        cm = mark(V.tensor_scalar(T.cmp[:, 1:512:4], T.ar[:, 0:128], T.ac[:, 1:2], nfb[:, 1:2], A.is_lt, A.is_gt))
-        mark(V.tensor_scalar(T.cmp[:, 513:4 * P:4], T.ar[:, 128:P], T.ac[:, 0:1], nfb[:, 0:1], A.is_le, A.is_gt), into=cm)
-        wait(V, sg)
-        mark(V.tensor_tensor(T.cmp[:, 0:4 * P:4], T.sg[:], thr[:], A.is_ge), into=cm)
-        wait(V, cm)
+        mark(S.activation(T.ch[:, 256:2 * P:2], T.ar[:, 128:P], F.Sign, bias=T.ac[:, 1:2], scale=-1.0), into=sg)
+        wait(V, aa, ar)
+        cm = mark(V.tensor_scalar(T.cmp[:, 513:4 * P:4], T.ar[:, 128:P], T.ac[:, 0:1], nfb[:, 0:1], A.is_le, A.is_gt))
+        wait(V, ab)
+        mark(V.tensor_scalar(T.cmp[:, 1:512:4], T.ar[:, 0:128], T.ac[:, 1:2], nfb[:, 1:2], A.is_lt, A.is_gt), into=cm)
+        wait(V, hi, sg)
+        mark(V.tensor_tensor_scan(T.cmp[:, 0:4 * P:2], T.cl[:], T.ch[:], 0.0, A.max, A.min), into=cm)
+        if first:
+            wait(V, high, low)
+            wait(PE, wk)
+        wait(V, rows, cm)
         kq = mark(quant("kk", 0, P, T.cmp[:]))
         wait(PE, kq)
-        z = mark(mm(T.pu0[:, 0:P], pair("wk"), pair("kk")))
+        z = mark(mm(T.pb[:, 0:P], pair("wk"), pair("kk")))
         if first:
-            za = mark(mm(T.pu1[:, 0:128], pair("kk", 0, 128), pair("wk")))
-            zc = mark(mm(T.pu2[:, 0:128], pair("kk", 32, P), pair("wk")))
+            za = mark(mm(T.pc[:, 0:128], pair("kk", 0, 128), pair("wk")))
+            zc = mark(mm(T.pd[:, 0:128], pair("kk", 32, P), pair("wk")))
         wait(V, z)
-        pl = mark(V.tensor_reduce(pc[:, 0:1], T.pu0[:, 0:P], AxisListType.X, A.min, apply_absolute_value=True))
-        wait(V, pl)
-        of = mark(V.tensor_copy(off[:, 0:1], pc[:, 0:1]))
+        if DIRECT:
+            of = mark(V.tensor_reduce(off[:, 0:1], T.pb[:, 0:P], AxisListType.X, A.min, apply_absolute_value=True))
+        else:
+            pl = mark(V.tensor_reduce(pc[:, 0:1], T.pb[:, 0:P], AxisListType.X, A.min, apply_absolute_value=True))
+            wait(V, pl)
+            of = mark(V.tensor_copy(off[:, 0:1], pc[:, 0:1]))
 
-        a, b = K * rank, K * rank + K
-        mq, ms = pair(mn, a, b)
+        mq, ms = pair(mn, K * rank, K * rank + K)
         wait(S, of)
         gs = mark(S.activation(ms, T[xn + "s"][:, 0:P].indirect(off[:, 0:1]), F.Copy))
         wait(V, of)
         gq = mark(V.tensor_copy(mq.bitcast(dt.uint32), T[xn + "q"][:, 0:P].bitcast(dt.uint32).indirect(off[:, 0:1])))
-        e_s, e_q = (engines[:half], engines[half:]) if first else (engines, engines)
-        to = near if GRID else others
-        arr = T.sem["arr%d" % t]
-        if first:
-            wait(g, em)
+        if DIRECT:
+            pl = mark(V.tensor_copy(pc[:, 0:1], off[:, 0:1]))
+        arr = "arr%d" % t
+        e_q, e_s = (engines[half:], engines[:half]) if first and SPLIT else (engines, engines)
         wait(g, gq)
-        sent[0] += put(to, mq.bitcast(dt.uint8), e_q, arr)
+        n = put(others, mq.bitcast(dt.uint8), arr, e_q)
         wait(g, gs)
-        sent[0] += put(to, ms, e_s, arr)
-        landed = ["arr%d" % t, len(to) * (len(e_s) + len(e_q))]
-        if GRID:
-            wait(g, landed)
-            mate = [cores[(rank + len(block)) % N]]
-            bq, bs = pair(mn, K * block[0], K * (block[-1] + 1))
-            far = T.sem["far%d" % t]
-            n = put(mate, bq.bitcast(dt.uint8), engines[half:], far) + put(mate, bs, engines[:half], far)
-            sent[0] += n
-            beyond = ["far%d" % t, n]
-        else:
-            beyond = None
+        landed = [arr, n + put(others, ms, arr, e_s)]
 
         if first:
+            wait(V, ez)
+            em = mark(V.tensor_scalar(T.em[:, 3:515:4], T.jp[:], 0.0, -4.0, A.is_equal, A.mult))
+            two = mark(V.memset(T.two[:], 2.0))
+            tab = mark(V.tensor_scalar(T.eye[:], T.jp[:], 0.0, None, A.is_equal))
             wait(V, em)
             eq = mark(quant("ee", 0, 128, T.em[:, 3:515]))
             for j in range(1, 4):
                 mark(quant("ee", 128 * j, 128 * j + 128, T.em[:, 3 - j:515 - j]), into=eq)
-            two = mark(V.memset(T.two[:], 2.0))
-            tab = mark(V.tensor_scalar(T.eye[:], T.jp[:], 0.0, None, A.is_equal))
             wait(V, two)
             mark(V.tensor_tensor_scan(T.up[:], T.two[:], T.zb[:, 0:NT], 2.0 ** LO, A.mult, A.add), into=tab)
             wait(V, w_in)
             wq = mark(quant("ww", 0, 128, T.wt[:]))
             cz = mark(S.activation(T.ct[:, 0:512], T.zb[:, 0:512], F.Copy))
             mark(S.activation(T.ct[:, 512:4 * P], T.zb[:, 0:4 * P - 512], F.Copy), into=cz)
-            rows = mark(V.tensor_scalar(T.cmp[0:1, 3:4 * P:4], T.pu0[0:1, 0:P], float(OUT), None, A.is_ge))
+            for j in range(4):
+                mark(S.activation(T.mt[:, 512 * j:512 * j + 512], T.zb[:, 0:512], F.Copy), into=cz)
+            rows = mark(V.tensor_scalar(T.cmp[0:1, 3:4 * P:4], T.pb[0:1, 0:P], float(OUT), None, A.is_ge))
             wait(V, za)
-            nf = mark(V.tensor_scalar(T.nf1[:, 0:1], T.pu1[:, 0:1], float(OUT), None, A.is_lt))
+            nf = mark(V.tensor_scalar(T.nf1[:, 0:1], T.pc[:, 0:1], float(OUT), None, A.is_lt))
             wait(V, zc)
-            mark(V.tensor_scalar(T.nf1[:, 1:2], T.pu2[:, 0:1], float(OUT), T.nf0[:, 1:2], A.is_lt, A.max), into=nf)
+            mark(V.tensor_scalar(T.nf1[:, 1:2], T.pd[:, 0:1], float(OUT), T.nf0[:, 1:2], A.is_lt, A.max), into=nf)
             wait(V, nf)
-            th = mark(V.tensor_scalar(T.th1[:, 0:128], T.th0[:, 0:128], T.nf1[:, 0:1], T.nf1[:, 0:1], A.add, A.add))
-            mark(V.tensor_scalar(T.th1[:, 128:P], T.th0[:, 96:128], T.nf1[:, 1:2], T.nf1[:, 1:2], A.add, A.add), into=th)
-            wait(V, tab, rows, th)
+            hi = upper(T.nf1)
+            wait(V, tab)
             wait(PE, eq)
-            wait(S, mz, cz)
-        banks = [T.pr0, T.pr1, T.pm, T.pg]
-
-        def decode(j):
+            wait(S, cz)
+        for j in range(4):
             mm(banks[j][:, 0:P], pair("ee", 128 * j, 128 * j + 128), pair(xn), True, False)
-
-        decode(0)
-        decode(1)
         if first:
-            wait(PE, wq, nf)
+            wait(PE, wq, nf, rows)
 
-        wait(PE, gq, gs, landed, beyond)
-        mmx = mark(mm(T.pm[:, 0:128], pair(mn), pair(mn)))
-        mtp = mark(mm(T.pt[:, 0:512], pair(mn), pair("ee")))
-        gp = mark(mm(T.pg[:, 0:P], pair(mn), pair(xn)))
-        yp = mark(mm(T.pu1[:, 0:128], pair("ww"), pair(mn)))
+        wait(PE, yc, pl, gq, gs, landed)
+        mmx = mark(mm(T.pa[:, 0:128], pair(mn), pair(mn)))
+        ta = mark(mm(T.pb[:, 0:256], pair(mn), pair("ee", 0, 256)))
+        gp = mark(mm(T.pc[:, 0:P], pair(mn), pair(xn)))
+        tb = mark(mm(T.pd[:, 0:256], pair(mn), pair("ee", 256, 512)))
 
         wait(V, mmx)
-        dg = mark(V.tensor_tensor(T.dg[:], T.pm[:, 0:128], T.eye[:], A.mult))
+        dg = mark(V.tensor_tensor(T.dg[0:64, :], T.pa[0:64, 0:64], T.eye[0:64, 0:64], A.mult))
+        mark(V.tensor_tensor(T.dg[64:128, :], T.pa[64:128, 64:128], T.eye[64:128, 64:128], A.mult), into=dg)
         wait(V, dg)
         dd = mark(V.tensor_reduce(T.dd[:, 0:1], T.dg[:], AxisListType.X, A.add))
         wait(V, dd)
         hm = mark(V.tensor_scalar(T.hm[:], T.up[:], T.dd[:, 0:1], 0.5, A.is_gt, A.max))
         wait(V, hm)
-        hh = mark(V.tensor_tensor_scan(T.hh[:], T.hm[:], T.zb[:, 0:NT], 2.0 ** -LO, A.mult, A.add))
+        hh = mark(V.tensor_tensor_scan(T.hh[:], T.hm[:, 0:NT // 2], T.hm[:, NT // 2:NT], 2.0 ** -LO, A.mult, A.mult))
         wait(PE, dg)
-        decode(2)
+        yp = mark(mm(T.pa[:, 0:128], pair("ww"), pair(mn)))
 
-        def turn(j):
-            o = 512 * (j % 2)
-            return mark(S.activation(T.mt[:, o:o + 512:4], T.pt[:, 128 * j:128 * j + 128], F.Copy, scale=-0.25))
+        def turn(j, n, src):
+            return mark(S.activation(T.mt[:, 512 * j:512 * (j + n):4], src, F.Copy, scale=-0.25))
 
-        def pack(j, made):
-            o = 512 * (j % 2)
+        def pack(j, n, made):
             wait(V, made)
-            return mark(quant("tt", 128 * j, 128 * j + 128, T.mt[:, o:o + 512]))
+            return mark(quant("tt", 128 * j, 128 * (j + n), T.mt[:, 512 * j:512 * (j + n)]))
 
-        wait(S, mtp)
-        m0 = turn(0)
-        m1 = turn(1)
+        wait(S, ta)
+        m01 = turn(0, 2, T.pb[:, 0:256])
         wait(S, gp, hh)
-        ct = mark(S.activation(T.ct[:, 0:4 * P:4], T.pg[:, 0:P], F.Copy, scale=T.hh[:, NT - 1:NT]))
-        wait(PE, ct)
-        decode(3)
-        q0 = pack(0, m0)
-        q1 = pack(1, m1)
+        ct = mark(S.activation(T.ct[:, 0:4 * P:4], T.pc[:, 0:P], F.Copy, scale=T.hh[:, NT // 2 - 1:NT // 2]))
+        wait(S, tb)
+        m2 = turn(2, 1, T.pd[:, 0:128])
+        m3 = turn(3, 1, T.pd[:, 128:256])
+        q01 = pack(0, 2, m01)
         wait(V, ct)
         cq = mark(quant("cc", 0, P, T.ct[:]))
-        wait(S, q0)
-        m2 = turn(2)
-        wait(S, q1)
-        m3 = turn(3)
-        q2 = pack(2, m2)
-        q3 = pack(3, m3)
+        q2 = pack(2, 1, m2)
+        q3 = pack(3, 1, m3)
         ys = T["ys%d" % t]
         wait(S, yp)
-        yc = mark(S.activation(ys[:], T.pu1[:, 0:128], F.Copy))
-        wait(Y, pl, landed, beyond)
+        yc = mark(S.activation(ys[:], T.pa[:, 0:128], F.Copy))
+        wait(Y, pl, landed)
         stores.append((Y, mark(Y.dma_start(T.pl[0:1, K * t:K * t + K], pc[0:K, 0:1]), 16)))
         wait(Y, yc)
         stores.append((Y, mark(Y.dma_start(T.y[:, 128 * t:128 * t + 128], ys[:]), 16)))
 
-        wait(PE, q0, q1, cq)
+        wait(PE, q01, cq)
         made = None
         for j, qj in enumerate((None, None, q2, q3)):
             wait(PE, qj)
@@ -315,7 +303,6 @@ def rank_program(g, core, T, topo):
                 made = mark(V.tensor_scalar(out, banks[j][:, 0:P], -0.25, None, A.mult), into=made)
         wait(V, made)
         xq = mark(quant("x%d" % (t + 1), 0, P, T.rt[:]))
-        u_free = [rows, yc, m3] if first else []
 
     wait(Y, xq)
     wait(S, xq)

from concourse.bass import DstId, RemoteDMATransfer
from concourse.mybir import dt, AluOpType, AxisListType, ActivationFunctionType

P, K, R, N = 160, 16, 2, 8
STEP = 512
OUT = STEP * K
LO, HI = -64, 72
NT = HI - LO
DIRECT = True
SPLIT = False

BF, F32, Q4, U8 = "bfloat16", "float32", "float8_e4m3fn_x4", "uint8"
SCRATCH = {
    "xt": ("sbuf", [128, 4 * P], BF), "ub": ("sbuf", [128, 8], BF), "wt": ("sbuf", [128, 512], BF),
    "zb": ("sbuf", [128, 528], BF), "jp": ("sbuf", [128, 128], BF), "ut": ("sbuf", [128, 512], BF),
    "cmp": ("sbuf", [128, 4 * P], BF), "wr": ("sbuf", [128, 512], BF), "em": ("sbuf", [128, 528], BF),
    "cl": ("sbuf", [128, 2 * P], BF), "ch": ("sbuf", [128, 2 * P], BF),
    "nf0": ("sbuf", [128, 4], F32), "nf1": ("sbuf", [128, 4], F32),
    "ar": ("sbuf", [128, P], F32), "ac": ("sbuf", [128, 4], F32),
    "pc0": ("sbuf", [128, 4], F32), "pc1": ("sbuf", [128, 4], F32),
    "off0": ("sbuf", [128, 8], "uint16"), "off1": ("sbuf", [128, 8], "uint16"),
    "eye": ("sbuf", [128, 128], BF), "two": ("sbuf", [128, NT], BF), "up": ("sbuf", [128, NT], BF),
    "dg": ("sbuf", [128, 64], F32), "dd": ("sbuf", [128, 4], F32), "hm": ("sbuf", [128, NT], BF),
    "hh": ("sbuf", [128, NT // 2], F32),
    "mt": ("sbuf", [128, 2048], BF), "ct": ("sbuf", [128, 4 * P], BF), "rt": ("sbuf", [128, 4 * P], BF),
    "ys0": ("sbuf", [128, 128], F32), "ys1": ("sbuf", [128, 128], F32),
    "pa": ("psum", [128, 512], F32), "pb": ("psum", [128, 512], F32), "pc": ("psum", [128, 512], F32),
    "pd": ("psum", [128, 512], F32), "pr0": ("psum", [128, 512], F32), "pr1": ("psum", [128, 512], F32),
    "pr2": ("psum", [128, 512], F32), "pr3": ("psum", [128, 512], F32),
}
for _n, _w in (("x0", P), ("x1", P), ("x2", P), ("m0", 128), ("m1", 128), ("uu", 128), ("ww", 128), ("wk", 128),
               ("kk", P), ("ee", 512), ("tt", 512), ("cc", P)):
    SCRATCH[_n + "q"] = ("sbuf", [128, _w], Q4)
    SCRATCH[_n + "s"] = ("sbuf", [128, _w], U8)

SEMAPHORES = ["arr0", "arr1", "sent"] + ["s%d" % i for i in range(140)]


def mask_of(engines):
    m = 0
    for e in engines:
        m |= 1 << e
    return m


def rank_program(g, core, T, topo):
    rank = T.rank_of(core)
    if rank is None:
        return
    A, F = AluOpType, ActivationFunctionType
    V, S, PE, Y = g.vector, g.scalar, g.tensor, g.sync
    used = [0]
    open_marks = {}

    def mark(ins, n=1, into=None):
        if into is None:
            into = ["s%d" % used[0], 0]
            used[0] += 1
        ins.then_inc(T.sem[into[0]], n)
        into[1] += n
        open_marks[into[0]] = into
        return into

    def wait(q, *marks):
        for m in marks:
            if m is not None:
                q.wait_ge(T.sem[m[0]], m[1])
                open_marks.pop(m[0], None)

    def pair(name, a=None, b=None):
        return T[name + "q"][:, a:b], T[name + "s"][:, a:b]

    def quant(name, a, b, src):
        q, s = pair(name, a, b)
        return V.quantize_mx(q, s, src)

    def mm(out, w, x, start=True, stop=True):
        return PE.matmul_mx(out, w[0], w[1], x[0], x[1], start, stop)

    def count(out, pattern, base, step):
        m = mark(g.iota(out, pattern, base, step, allow_small_or_imprecise_dtypes=True))
        wait(g, m)
        return m

    cores = list(T.cores)
    others = [cores[(rank + i) % N] for i in range(1, N)]
    engines = [e for e in topo.engines(core, others[0]) if all(e in topo.engines(core, c) for c in others)]
    half = len(engines) // 2
    sent = [0]

    def put(dsts, src, sem, use):
        ids = []
        for c in dsts:
            rid, pid, _ = topo.addr(c)
            ids.append(DstId(rid=rid, pnc=pid))
        tr = RemoteDMATransfer(dst_ids=ids, dma_engine_mask=mask_of(use), remote_sem=T.sem[sem], src=src,
                               dsts=[src for _ in dsts])
        g.remote_dma_fused([tr], local_sem=T.sem.sent)
        sent[0] += len(use)
        return len(dsts) * len(use)

    u_in = mark(S.dma_start(T.ub[:, 0:4], T.u[:]), 16)
    x_in = mark(Y.dma_start(T.xt[:], T.x[:]), 16)
    wait(Y, x_in)
    w_in = mark(Y.dma_start(T.wt[:], T.w[:]), 16)

    wz = mark(V.memset(T.wr[:, 3:512:4], 0.0))
    zb = mark(V.memset(T.zb[:], 0.0))
    jp = count(T.jp[:], [[1, 128]], 0, -1)
    wr = mark(V.memset(T.wr[:, 0:512:4], 0.0))
    mark(V.memset(T.wr[:, 1:512:4], float(STEP)), into=wr)
    mark(V.memset(T.wr[:, 2:512:4], float(STEP)), into=wr)
    wait(V, wz)
    w2 = mark(V.memset(T.wr[64:66, 3:512:4], 16.0 * STEP))
    mark(V.memset(T.wr[96:98, 3:512:4], float(STEP)), into=w2)
    mark(V.memset(T.wr[0:1, 3:512:4], float(-OUT)), into=wr)
    rows = mark(V.memset(T.cmp[0:64, 3:4 * P:4], 1.0))
    wait(g, wz)
    krow = count(T.wr[32:33, 3:512:4], [[0, 128 // K], [-STEP, K]], OUT, 0)
    high = count(T.cmp[64:96, 3:4 * P:4], [[1, P // 16], [0, 16]], 0, 0)
    low = count(T.cmp[96:128, 3:4 * P:4], [[0, P // 16], [1, 16]], 0, 0)
    lo = mark(V.memset(T.cl[:, 0:2 * P:2], 2.0))
    mark(V.memset(T.cl[0:64, 257:2 * P:2], -1.5), into=lo)
    wait(V, jp)
    mark(V.tensor_scalar(T.cl[:, 1:256:2], T.jp[:], 0.0, -1.0, A.is_gt, A.mult), into=lo)
    mark(V.tensor_scalar(T.cl[64:128, 257:2 * P:2], T.jp[64:128, 96:128], 0.0, -1.0, A.is_gt, A.mult), into=lo)
    mark(V.tensor_scalar(T.nf0[:, 0:2], T.jp[:, 0:97:96], 0.0, None, A.is_gt), into=lo)

    def upper(nfb):
        m = mark(V.tensor_scalar(T.ch[:, 1:256:2], T.cl[:, 1:256:2], nfb[:, 0:1], 1.0, A.subtract, A.add))
        return mark(V.tensor_scalar(T.ch[:, 257:2 * P:2], T.cl[:, 257:2 * P:2], nfb[:, 1:2], 1.0, A.subtract, A.add), into=m)

    wait(S, zb)
    ez = mark(S.activation(T.em[:, 0:516], T.zb[:, 0:516], F.Copy))

    wait(S, u_in)
    ut = mark(S.activation(T.ut[:, 0:512:4], T.zb[:, 0:128], F.Identity, bias=T.ub[:, 0:1]))
    wait(V, zb, u_in)
    for j in range(1, 4):
        mark(V.tensor_scalar(T.ut[:, j:512:4], T.zb[:, 0:128], T.ub[:, j:j + 1], None, A.add), into=ut)
    wait(V, w2)
    mark(V.memset(T.wr[64:65, 3:512:4], 16.0), into=wr)
    mark(V.memset(T.wr[96:97, 3:512:4], 1.0), into=wr)
    wait(V, ut)
    uq = mark(quant("uu", 0, 128, T.ut[:]))
    wait(V, x_in)
    xq = mark(quant("x0", 0, P, T.xt[:]))
    wait(PE, uq)
    wait(V, lo)
    hi = upper(T.nf0)
    wait(V, wr, krow)
    wk = mark(quant("wk", 0, 128, T.wr[:]))

    stores = []
    banks = [T.pr0, T.pr1, T.pr2, T.pr3]
    yc = None
    for t in range(R):
        xn, mn = "x%d" % t, "m%d" % t
        nfb, pc, off = T["nf%d" % t], T["pc%d" % t], T["off%d" % t]
        first = t == 0

        wait(PE, xq)
        row = mark(mm(T.pb[:, 0:P], pair("uu"), pair(xn)))
        ca = mark(mm(T.pc[:, 0:128], pair(xn, 0, 128), pair("uu")))
        cb = mark(mm(T.pd[:, 0:128], pair(xn, 32, P), pair("uu")))
        wait(S, row)
        ar = mark(S.activation(T.ar[:], T.pb[:, 0:P], F.Abs))
        wait(V, ca)
        aa = mark(V.tensor_scalar(T.ac[:, 0:1], T.pc[:, 0:1], -1.0, T.pc[:, 0:1], A.mult, A.max))
        wait(V, cb)
        ab = mark(V.tensor_scalar(T.ac[:, 1:2], T.pd[:, 0:1], -1.0, T.pd[:, 0:1], A.mult, A.max))

        wait(S, aa, ar)
        sg = mark(S.activation(T.ch[:, 0:256:2], T.ar[:, 0:128], F.Sign, bias=T.ac[:, 0:1], scale=-1.0))
        wait(S, ab)
        mark(S.activation(T.ch[:, 256:2 * P:2], T.ar[:, 128:P], F.Sign, bias=T.ac[:, 1:2], scale=-1.0), into=sg)
        wait(V, aa, ar)
        cm = mark(V.tensor_scalar(T.cmp[:, 513:4 * P:4], T.ar[:, 128:P], T.ac[:, 0:1], nfb[:, 0:1], A.is_le, A.is_gt))
        wait(V, ab)
        mark(V.tensor_scalar(T.cmp[:, 1:512:4], T.ar[:, 0:128], T.ac[:, 1:2], nfb[:, 1:2], A.is_lt, A.is_gt), into=cm)
        wait(V, hi, sg)
        mark(V.tensor_tensor_scan(T.cmp[:, 0:4 * P:2], T.cl[:], T.ch[:], 0.0, A.max, A.min), into=cm)
        if first:
            wait(V, high, low)
            wait(PE, wk)
        wait(V, rows, cm)
        kq = mark(quant("kk", 0, P, T.cmp[:]))
        wait(PE, kq)
        z = mark(mm(T.pb[:, 0:P], pair("wk"), pair("kk")))
        if first:
            za = mark(mm(T.pc[:, 0:128], pair("kk", 0, 128), pair("wk")))
            zc = mark(mm(T.pd[:, 0:128], pair("kk", 32, P), pair("wk")))
        wait(V, z)
        if DIRECT:
            of = mark(V.tensor_reduce(off[:, 0:1], T.pb[:, 0:P], AxisListType.X, A.min, apply_absolute_value=True))
        else:
            pl = mark(V.tensor_reduce(pc[:, 0:1], T.pb[:, 0:P], AxisListType.X, A.min, apply_absolute_value=True))
            wait(V, pl)
            of = mark(V.tensor_copy(off[:, 0:1], pc[:, 0:1]))

        mq, ms = pair(mn, K * rank, K * rank + K)
        wait(S, of)
        gs = mark(S.activation(ms, T[xn + "s"][:, 0:P].indirect(off[:, 0:1]), F.Copy))
        wait(V, of)
        gq = mark(V.tensor_copy(mq.bitcast(dt.uint32), T[xn + "q"][:, 0:P].bitcast(dt.uint32).indirect(off[:, 0:1])))
        if DIRECT:
            pl = mark(V.tensor_copy(pc[:, 0:1], off[:, 0:1]))
        arr = "arr%d" % t
        e_q, e_s = (engines[half:], engines[:half]) if first and SPLIT else (engines, engines)
        wait(g, gq)
        n = put(others, mq.bitcast(dt.uint8), arr, e_q)
        wait(g, gs)
        landed = [arr, n + put(others, ms, arr, e_s)]

        if first:
            wait(V, ez)
            em = mark(V.tensor_scalar(T.em[:, 3:515:4], T.jp[:], 0.0, -4.0, A.is_equal, A.mult))
            two = mark(V.memset(T.two[:], 2.0))
            tab = mark(V.tensor_scalar(T.eye[:], T.jp[:], 0.0, None, A.is_equal))
            wait(V, em)
            eq = mark(quant("ee", 0, 128, T.em[:, 3:515]))
            for j in range(1, 4):
                mark(quant("ee", 128 * j, 128 * j + 128, T.em[:, 3 - j:515 - j]), into=eq)
            wait(V, two)
            mark(V.tensor_tensor_scan(T.up[:], T.two[:], T.zb[:, 0:NT], 2.0 ** LO, A.mult, A.add), into=tab)
            wait(V, w_in)
            wq = mark(quant("ww", 0, 128, T.wt[:]))
            cz = mark(S.activation(T.ct[:, 0:512], T.zb[:, 0:512], F.Copy))
            mark(S.activation(T.ct[:, 512:4 * P], T.zb[:, 0:4 * P - 512], F.Copy), into=cz)
            for j in range(4):
                mark(S.activation(T.mt[:, 512 * j:512 * j + 512], T.zb[:, 0:512], F.Copy), into=cz)
            rows = mark(V.tensor_scalar(T.cmp[0:1, 3:4 * P:4], T.pb[0:1, 0:P], float(OUT), None, A.is_ge))
            wait(V, za)
            nf = mark(V.tensor_scalar(T.nf1[:, 0:1], T.pc[:, 0:1], float(OUT), None, A.is_lt))
            wait(V, zc)
            mark(V.tensor_scalar(T.nf1[:, 1:2], T.pd[:, 0:1], float(OUT), T.nf0[:, 1:2], A.is_lt, A.max), into=nf)
            wait(V, nf)
            hi = upper(T.nf1)
            wait(V, tab)
            wait(PE, eq)
            wait(S, cz)
        for j in range(4):
            mm(banks[j][:, 0:P], pair("ee", 128 * j, 128 * j + 128), pair(xn), True, False)
        if first:
            wait(PE, wq, nf, rows)

        wait(PE, yc, pl, gq, gs, landed)
        mmx = mark(mm(T.pa[:, 0:128], pair(mn), pair(mn)))
        ta = mark(mm(T.pb[:, 0:256], pair(mn), pair("ee", 0, 256)))
        gp = mark(mm(T.pc[:, 0:P], pair(mn), pair(xn)))
        tb = mark(mm(T.pd[:, 0:256], pair(mn), pair("ee", 256, 512)))

        wait(V, mmx)
        dg = mark(V.tensor_tensor(T.dg[0:64, :], T.pa[0:64, 0:64], T.eye[0:64, 0:64], A.mult))
        mark(V.tensor_tensor(T.dg[64:128, :], T.pa[64:128, 64:128], T.eye[64:128, 64:128], A.mult), into=dg)
        wait(V, dg)
        dd = mark(V.tensor_reduce(T.dd[:, 0:1], T.dg[:], AxisListType.X, A.add))
        wait(V, dd)
        hm = mark(V.tensor_scalar(T.hm[:], T.up[:], T.dd[:, 0:1], 0.5, A.is_gt, A.max))
        wait(V, hm)
        hh = mark(V.tensor_tensor_scan(T.hh[:], T.hm[:, 0:NT // 2], T.hm[:, NT // 2:NT], 2.0 ** -LO, A.mult, A.mult))
        wait(PE, dg)
        yp = mark(mm(T.pa[:, 0:128], pair("ww"), pair(mn)))

        def turn(j, n, src):
            return mark(S.activation(T.mt[:, 512 * j:512 * (j + n):4], src, F.Copy, scale=-0.25))

        def pack(j, n, made):
            wait(V, made)
            return mark(quant("tt", 128 * j, 128 * (j + n), T.mt[:, 512 * j:512 * (j + n)]))

        wait(S, ta)
        m01 = turn(0, 2, T.pb[:, 0:256])
        wait(S, gp, hh)
        ct = mark(S.activation(T.ct[:, 0:4 * P:4], T.pc[:, 0:P], F.Copy, scale=T.hh[:, NT // 2 - 1:NT // 2]))
        wait(S, tb)
        m2 = turn(2, 1, T.pd[:, 0:128])
        m3 = turn(3, 1, T.pd[:, 128:256])
        q01 = pack(0, 2, m01)
        wait(V, ct)
        cq = mark(quant("cc", 0, P, T.ct[:]))
        q2 = pack(2, 1, m2)
        q3 = pack(3, 1, m3)
        ys = T["ys%d" % t]
        wait(S, yp)
        yc = mark(S.activation(ys[:], T.pa[:, 0:128], F.Copy))
        wait(Y, pl, landed)
        stores.append((Y, mark(Y.dma_start(T.pl[0:1, K * t:K * t + K], pc[0:K, 0:1]), 16)))
        wait(Y, yc)
        stores.append((Y, mark(Y.dma_start(T.y[:, 128 * t:128 * t + 128], ys[:]), 16)))

        wait(PE, q01, cq)
        made = None
        for j, qj in enumerate((None, None, q2, q3)):
            wait(PE, qj)
            zj = mark(mm(banks[j][:, 0:P], pair("tt", 128 * j, 128 * j + 128), pair("cc"), False, True))
            out = T.rt[:, j:4 * P:4]
            if j % 2 == 0:
                wait(S, zj)
                made = mark(S.activation(out, banks[j][:, 0:P], F.Copy, scale=-0.25), into=made)
            else:
                wait(V, zj)
                made = mark(V.tensor_scalar(out, banks[j][:, 0:P], -0.25, None, A.mult), into=made)
        wait(V, made)
        xq = mark(quant("x%d" % (t + 1), 0, P, T.rt[:]))

    wait(Y, xq)
    wait(S, xq)
    last_q, last_s = T["x%dq" % R], T["x%ds" % R]
    stores.append((Y, mark(Y.dma_start(T.oc[:], last_q[:].bitcast(dt.uint8)), 16)))
    for k in range(4):
        q = S if k < 3 else Y
        stores.append((q, mark(q.dma_start(T.osc[4 * k:4 * k + 4, :], last_s[32 * k:32 * k + 4, :]), 16)))
    g.wait_ge(T.sem.sent, sent[0])
    for q, m in stores:
        wait(q, m)
    for m in list(open_marks.values()):
        wait(g, m)
